import numpy as np
import ml_dtypes


def mxq(x, axis, fmt="e4m3"):
    dtype, down = {"e4m3": (ml_dtypes.float8_e4m3fn, 7), "e5m2": (ml_dtypes.float8_e5m2, 14)}[fmt]
    v = np.moveaxis(np.asarray(x, np.float32).astype(ml_dtypes.bfloat16).astype(np.float64), axis, -1)
    blocks = v.reshape(v.shape[:-1] + (-1, 32))
    amax = np.abs(blocks).max(-1, keepdims=True)
    byte = np.maximum(np.where(amax > 0, np.frexp(amax)[1] - 1 + 127, 0) - down, 1)
    scale = np.exp2(byte - 127.0)
    codes = (blocks / scale).astype(np.float32).astype(dtype).astype(np.float64)
    return np.moveaxis((codes * scale).reshape(v.shape), -1, axis)


WIDE = False


def mx_kscale(k):
    if not WIDE:
        return np.ones(k)
    levels = np.array([10, -10, 5, -5, 0])
    if k % 512:
        return np.exp2(np.random.permutation(np.resize(levels, k // 32))).repeat(32)
    a = np.empty((k // 512, 16))
    for p in range(k // 512):
        a[p, :8] = np.random.permutation(np.resize(levels, 8))
        for g in range(8):
            far = levels[np.abs(levels - a[p, g]) >= 10]
            a[p, g + 8] = far[np.random.randint(len(far))]
    return np.exp2(a.ravel()).repeat(32)


BF16 = ml_dtypes.bfloat16


def bf(x):
    return np.asarray(x, np.float32).astype(BF16)


def f64(x):
    return np.asarray(x).astype(np.float64)


E2M1 = np.array([0.0, 0.5, 1.0, 1.5, 2.0, 3.0, 4.0, 6.0, -0.0, -0.5, -1.0, -1.5, -2.0, -3.0, -4.0, -6.0])


def pack_weight(w, fmt):
    k, n = w.shape
    w = f64(bf(w)).reshape(k // 32, 32, n)
    amax = np.abs(w).max(1)
    if fmt == "e4m3":
        byte = np.frexp(amax)[1] - 1 + 127 - 7
    else:
        mant, ex = np.frexp(amax / 6.0)
        byte = np.where(mant > 0.5, ex, ex - 1) + 127
    byte = np.clip(np.where(amax > 0, byte, 1), 1, 254)
    scaled = (w * np.exp2(127.0 - byte)[:, None, :]).reshape(k, n).astype(np.float32)
    by_word = np.ascontiguousarray(scaled.reshape(k // 512, 128, 4, n).transpose(0, 1, 3, 2))
    if fmt == "e4m3":
        words = by_word.astype(ml_dtypes.float8_e4m3fn).view(np.uint8)
    else:
        c = by_word.astype(ml_dtypes.float4_e2m1fn).view(np.uint8) & 0xF
        words = c[..., 0::2] | (c[..., 1::2] << 4)
    return np.ascontiguousarray(words), np.ascontiguousarray(byte.astype(np.uint8).reshape(k // 512, 16, n))


def unpack_weight(words, scales, fmt):
    g, p, n, _ = words.shape
    if fmt == "e4m3":
        vals = np.ascontiguousarray(words).view(ml_dtypes.float8_e4m3fn).astype(np.float64)
    else:
        nib = np.empty((g, p, n, 4), np.uint8)
        nib[..., 0::2] = words & 0xF
        nib[..., 1::2] = words >> 4
        vals = E2M1[nib]
    vals = vals * np.repeat(np.exp2(scales.astype(np.float64) - 127.0), 8, axis=1)[..., None]
    return vals.transpose(0, 1, 3, 2).reshape(g * 512, n)
def pack4(w):
    words, scales = pack_weight(w, "e2m1")
    return words.reshape(words.shape[0], 128, -1), scales


def unpack4(words, scales):
    return unpack_weight(words.reshape(words.shape[0], 128, -1, 2), scales, "e2m1")


def planes(Y):
    n, m = Y.shape
    b = f64(bf(Y)).reshape(n // 32, 32, m)
    amax = np.abs(b).max(1)
    byte = np.clip(np.where(amax > 0, np.frexp(amax)[1] - 1 + 127 - 7, 1), 1, 254)
    codes = (b * np.exp2(127.0 - byte)[:, None, :]).reshape(n, m).astype(np.float32).astype(ml_dtypes.float8_e4m3fn).view(np.uint8)
    words = codes.reshape(n // 512, 128, 4, m).transpose(0, 1, 3, 2)
    return np.ascontiguousarray(words), np.ascontiguousarray(byte.astype(np.uint8).reshape(n // 512, 16, m))


S, K, F, N = 1024, 1024, 2048, 1024

SLOPE = 1.702


def setup_inputs():
    s = mx_kscale(K)
    t = mx_kscale(F)
    draws = np.random.randn(S, K)
    L = np.random.randn(K, F) + 0.6 * np.random.randn(K, 1)
    L = L / np.sqrt((L ** 2).sum(axis=0, keepdims=True))
    severity = np.exp(0.5 * np.random.randn(F))
    size = np.exp(0.5 * np.random.randn(N))
    H = np.random.randn(F, N) * size[None, :] / np.sqrt(F)
    factor_words, factor_scales = pack4(L / s[:, None])
    shares_words, shares_scales = pack4(H / t[:, None])
    return {"draws": bf(draws * s[None, :]),
            "factor_words": factor_words, "factor_scales": factor_scales,
            "severity": bf(severity * t),
            "shares_words": shares_words, "shares_scales": shares_scales,
            "claims_index": bf(np.exp(0.8 * np.random.randn(S))),
            "expense": bf(0.3 * size * np.exp(0.3 * np.random.randn(N)))}


def reference(draws, factor_words, factor_scales, severity, shares_words, shares_scales, claims_index, expense):
    L = unpack4(factor_words, factor_scales)
    H = unpack4(shares_words, shares_scales)
    x = mxq(f64(draws), 1, "e4m3") @ L
    loss = f64(severity)[None, :] / (1.0 + np.exp(-SLOPE * x))
    net = mxq(loss, 1, "e4m3") @ H
    y = f64(claims_index)[:, None] * net + f64(expense)[None, :]
    Y = y.reshape(S, N)
    words, scales = planes(Y)
    return y, words, scales

@@ -1,0 +1,304 @@
+from contextlib import ExitStack
+
+import concourse.mybir as mybir
+from concourse.masks import make_identity
+
+S, K, F, N = 1024, 1024, 2048, 1024
+SLOPE = 1.702
+FLOPS = 2 * S * K * F + 2 * S * F * N
+
+F32 = mybir.dt.float32
+BF16 = mybir.dt.bfloat16
+I32 = mybir.dt.int32
+U32 = mybir.dt.uint32
+U8 = mybir.dt.uint8
+FP8X4 = mybir.dt.float8_e4m3fn_x4
+FP4X4 = mybir.dt.float4_e2m1fn_x4
+ALU = mybir.AluOpType
+ACT = mybir.ActivationFunctionType
+
+P = 128
+PACK = 4
+PASS = P * PACK
+HALVES = S // PASS
+K_PASSES = K // PASS
+F_PASSES = F // PASS
+N_HALVES = N // PASS
+RUN = 4
+
+
+def tile_correlated_insurer_losses_h1_kernel(
+    tc, draws, factor_words, factor_scales, severity, shares_words, shares_scales, claims_index, expense,
+    out_0, out_1, out_2,
+):
+    nc = tc.nc
+    with ExitStack() as ctx:
+        keep = ctx.enter_context(tc.tile_pool(name="keep", bufs=1))
+        work = ctx.enter_context(tc.tile_pool(name="work", bufs=2))
+        psum = ctx.enter_context(tc.psum_pool(name="psum", bufs=1))
+        ctx.enter_context(tc.manual_schedule())
+
+        ident = keep.tile([P, P], F32, align_bytes=64)
+        draws_raw = keep.tile([P, HALVES, K_PASSES, PACK, PASS], BF16, align_bytes=64)
+        draws_codes = keep.tile([P, HALVES, K_PASSES, PASS], U32, align_bytes=64)
+        draws_sc = keep.tile([P, HALVES, K_PASSES, PASS], U8, align_bytes=64)
+        l_raw = keep.tile([P, F_PASSES, K_PASSES, 2 * PASS], U8, align_bytes=64)
+        l_words = keep.tile([P, F_PASSES, K_PASSES, 2 * PASS], U8, align_bytes=64)
+        l_sc_raw = keep.tile([P, K_PASSES, F], U8, align_bytes=64)
+        l_sc = keep.tile([P, K_PASSES, F], U8, align_bytes=64)
+        h_words = keep.tile([P, F_PASSES, 2 * N], U8, align_bytes=64)
+        h_sc = keep.tile([P, F_PASSES, N], U8, align_bytes=64)
+        sev = keep.tile([P, F_PASSES, PACK], BF16, align_bytes=64)
+        index = keep.tile([P, HALVES, PACK], BF16, align_bytes=64)
+        cost = keep.tile([P, N], BF16, align_bytes=64)
+        loss_codes = keep.tile([P, HALVES, F_PASSES, PASS], U32, align_bytes=64)
+        loss_sc = keep.tile([P, HALVES, F_PASSES, PASS], U8, align_bytes=64)
+        y_codes = keep.tile([P, HALVES, N], U32, align_bytes=64)
+        y_sc = keep.tile([P, HALVES, N], U8, align_bytes=64)
+        warm = keep.tile([P, 2], F32, align_bytes=64)
+
+        live = {}
+
+        def bank(number, shape):
+            return psum.tile(shape, F32, name="bank%d" % number, tag="bank%d" % number)
+
+        def load_draws(h, g):
+            rows = draws[h * PASS : (h + 1) * PASS, g * PASS : (g + 1) * PASS]
+            nc.sync.dma_start(out=draws_raw[:, h, g, :, :], in_=rows.rearrange("(m t) k -> m t k", t=PACK))
+
+        def load_scale_rows(plane, source):
+            rows = source.bitcast(I32)
+            for q in range(4):
+                nc.sync.dma_start(
+                    out=plane[32 * q : 32 * q + 4, :, :].bitcast(I32),
+                    in_=rows[:, 4 * q : 4 * q + 4, :].rearrange("g r n -> r g n"),
+                )
+
+        def load_l(c):
+            part = factor_words.bitcast(I32)[:, :, c * 256 : (c + 1) * 256]
+            nc.sync.dma_start(out=l_raw[:, c, :, :].bitcast(I32), in_=part.rearrange("g p w -> p g w"))
+
+        def load_h(c):
+            nc.sync.dma_start(out=h_words[:, c, :].bitcast(I32), in_=shares_words.bitcast(I32)[c])
+
+        def permute_sc(c):
+            cols = slice(c * PASS, (c + 1) * PASS)
+            nc.vector.tensor_copy(
+                out=l_sc[:, :, cols].rearrange("p g (t m) -> p g t m", t=PACK),
+                in_=l_sc_raw[:, :, cols].rearrange("p g (m t) -> p g t m", t=PACK),
+            )
+
+        def permute_l(c):
+            nc.vector.tensor_copy(
+                out=l_words[:, c, :, :].rearrange("p g (t m b) -> p g t m b", t=PACK, b=2),
+                in_=l_raw[:, c, :, :].rearrange("p g (m t b) -> p g t m b", t=PACK, b=2),
+            )
+
+        def turn_draws(h, g):
+            grouped = work.tile([P, PASS, PACK], BF16, name="grouped", align_bytes=64)
+            live["grouped", h, g] = grouped
+            for a in range(2):
+                turned = bank(4 + 2 * g + a, [P, 2, 2, P])
+                for i in range(2):
+                    words = draws_raw[:, h, g, 2 * a + i, :].bitcast(F32)
+                    for u in range(2):
+                        nc.tensor.transpose(turned[:, i, u, :], words[:, u : 2 * P : 2], ident[:])
+                nc.scalar.copy(
+                    out=grouped[:, 2 * a * P : 2 * (a + 1) * P, :].bitcast(F32).rearrange("p (i r) u -> p i r u", i=2),
+                    in_=turned[:].rearrange("p i u r -> p i r u"),
+                )
+
+        def quantize_draws(h, g):
+            nc.vector.quantize_mx(
+                out=draws_codes[:, h, g, :].bitcast(FP8X4),
+                scales=draws_sc[:, h, g, :],
+                in_=live["grouped", h, g][:].rearrange("p s t -> p (s t)"),
+            )
+
+        def first_product(h, c, pass_major=False):
+            prob = work.tile([P, PACK, PASS], F32, name="prob", bufs=4, align_bytes=64)
+            live["prob", h, c] = prob
+            banks = [bank(t, [P, PASS]) for t in range(PACK)]
+            order = [(t, g) for t in range(PACK) for g in range(K_PASSES)]
+            if pass_major:
+                order = [(t, g) for g in range(K_PASSES) for t in range(PACK)]
+            for t, g in order:
+                nc.tensor.matmul_mx(
+                    out=banks[t][:],
+                    lhsT=l_words[:, c, g, 2 * P * t : 2 * P * (t + 1)].bitcast(FP4X4),
+                    lhsT_scale=l_sc[:, g, c * PASS + P * t : c * PASS + P * (t + 1)],
+                    rhs=draws_codes[:, h, g, :].bitcast(FP8X4),
+                    rhs_scale=draws_sc[:, h, g, :],
+                    start=(g == 0),
+                    stop=(g == K_PASSES - 1),
+                )
+                if g == K_PASSES - 1:
+                    nc.scalar.activation(out=prob[:, t, :], in_=banks[t][:], func=ACT.Sigmoid, scale=SLOPE)
+
+        def weigh(h, c):
+            loss = work.tile([P, PASS, PACK], BF16, name="loss", align_bytes=64)
+            live["loss", h, c] = loss
+            nc.vector.tensor_tensor(
+                out=loss[:].rearrange("p (s i) t -> p s t i", i=RUN),
+                in0=live["prob", h, c][:].rearrange("p t (s i) -> p s t i", i=RUN),
+                in1=sev[:, c, :].unsqueeze(1).unsqueeze(3).to_broadcast([P, PASS // RUN, PACK, RUN]),
+                op=ALU.mult,
+            )
+
+        def quantize_loss(h, c):
+            nc.vector.quantize_mx(
+                out=loss_codes[:, h, c, :].bitcast(FP8X4),
+                scales=loss_sc[:, h, c, :],
+                in_=live["loss", h, c][:].rearrange("p s t -> p (s t)"),
+            )
+
+        def second_pass(h, j, t, c, first_bank=4):
+            if c == 0:
+                live["net", h, j, t] = bank(first_bank + t, [P, PASS])
+            nc.tensor.matmul_mx(
+                out=live["net", h, j, t][:],
+                lhsT=loss_codes[:, h, c, P * t : P * (t + 1)].bitcast(FP8X4),
+                lhsT_scale=loss_sc[:, h, c, P * t : P * (t + 1)],
+                rhs=h_words[:, c, 2 * PASS * j : 2 * PASS * (j + 1)].bitcast(FP4X4),
+                rhs_scale=h_sc[:, c, PASS * j : PASS * (j + 1)],
+                start=(c == 0),
+                stop=(c == F_PASSES - 1),
+            )
+
+        def second_passes(h, j, c, first_bank=4):
+            for t in range(PACK):
+                second_pass(h, j, t, c, first_bank)
+
+        def finish(h, j, t):
+            if t == 0:
+                live["y", h, j] = work.tile([P, PACK, PASS], F32, name="y", bufs=3, align_bytes=64)
+            y = live["y", h, j]
+            cols = slice(j * PASS, (j + 1) * PASS)
+            nc.vector.scalar_tensor_tensor(
+                out=y[:, t, :], in0=live["net", h, j, t][:], scalar=index[:, h, t : t + 1], in1=cost[:, cols],
+                op0=ALU.mult, op1=ALU.add,
+            )
+            rows = out_0[h * PASS : (h + 1) * PASS, cols].rearrange("(p t) n -> p t n", t=PACK)
+            nc.sync.dma_start(out=rows[:, t, :], in_=y[:, t, :])
+
+        def round_y(h, j, split=PASS):
+            y = live["y", h, j]
+            rounded = work.tile([P, PASS, PACK], BF16, name="rounded", align_bytes=64)
+            live["rounded", h, j] = rounded
+            nc.scalar.copy(
+                out=rounded[:, :split, :].rearrange("p (n i) t -> p n t i", i=RUN),
+                in_=y[:, :, :split].rearrange("p t (n i) -> p n t i", i=RUN),
+            )
+            if split < PASS:
+                nc.vector.tensor_copy(
+                    out=rounded[:, split:, :].rearrange("p (n i) t -> p n t i", i=RUN),
+                    in_=y[:, :, split:].rearrange("p t (n i) -> p n t i", i=RUN),
+                )
+
+        def quantize_y(h, j):
+            cols = slice(j * PASS, (j + 1) * PASS)
+            nc.vector.quantize_mx(
+                out=y_codes[:, h, cols].bitcast(FP8X4),
+                scales=y_sc[:, h, cols],
+                in_=live["rounded", h, j][:].rearrange("p n t -> p (n t)"),
+            )
+            words = out_1[h].rearrange("p n t -> p (n t)").bitcast(I32)
+            nc.sync.dma_start(out=words[:, cols], in_=y_codes[:, h, cols].bitcast(I32))
+            if j == N_HALVES - 1:
+                rows = out_2[h].bitcast(I32)
+                for q in range(4):
+                    nc.sync.dma_start(out=rows[4 * q : 4 * q + 4, :], in_=y_sc[32 * q : 32 * q + 4, h, :].bitcast(I32))
+
+        nc.vector.memset(l_sc_raw[:].bitcast(I32), 0)
+        nc.vector.memset(h_sc[:].bitcast(I32), 0)
+        make_identity(nc, ident[:])
+        nc.scalar.activation(out=warm[:], in_=ident[:, 0:2], func=ACT.Sigmoid, scale=SLOPE)
+
+        load_draws(0, 0)
+        load_l(0)
+        load_scale_rows(l_sc_raw, factor_scales)
+        load_draws(0, 1)
+        load_l(1)
+        load_draws(1, 0)
+        nc.sync.dma_start(out=sev[:], in_=severity.rearrange("(c p t) -> p c t", p=P, t=PACK))
+        load_l(2)
+        load_draws(1, 1)
+        load_l(3)
+        load_scale_rows(h_sc, shares_scales)
+        for c in range(F_PASSES):
+            load_h(c)
+        nc.sync.dma_start(out=index[:], in_=claims_index.rearrange("(h p t) -> p h t", p=P, t=PACK))
+        nc.sync.dma_start(out=cost[:], in_=expense.partition_broadcast(P))
+
+        turn_draws(0, 0)
+        turn_draws(0, 1)
+        permute_l(0)
+        permute_sc(0)
+        quantize_draws(0, 0)
+        permute_sc(1)
+        permute_l(1)
+        quantize_draws(0, 1)
+        permute_sc(2)
+        permute_l(2)
+        permute_sc(3)
+        permute_l(3)
+        first_product(0, 0, pass_major=True)
+        turn_draws(1, 0)
+        first_product(0, 1)
+        turn_draws(1, 1)
+        weigh(0, 0)
+        quantize_draws(1, 0)
+        quantize_loss(0, 0)
+        first_product(0, 2)
+        second_passes(0, 0, 0)
+        weigh(0, 1)
+        quantize_draws(1, 1)
+        quantize_loss(0, 1)
+        first_product(0, 3)
+        second_passes(0, 0, 1)
+        weigh(0, 2)
+        quantize_loss(0, 2)
+        first_product(1, 0)
+        second_passes(0, 0, 2)
+        weigh(0, 3)
+        quantize_loss(0, 3)
+        first_product(1, 1)
+        second_passes(0, 0, 3)
+        weigh(1, 0)
+        finish(0, 0, 0)
+        quantize_loss(1, 0)
+        for t in range(1, PACK):
+            finish(0, 0, t)
+        first_product(1, 2)
+        for t in range(PACK):
+            for c in range(F_PASSES):
+                second_pass(0, 1, t, c)
+        round_y(0, 0)
+        weigh(1, 1)
+        finish(0, 1, 0)
+        quantize_loss(1, 1)
+        for t in range(1, PACK):
+            finish(0, 1, t)
+        first_product(1, 3)
+        second_passes(1, 0, 0)
+        second_passes(1, 0, 1)
+        round_y(0, 1)
+        weigh(1, 2)
+        quantize_y(0, 0)
+        quantize_loss(1, 2)
+        second_passes(1, 0, 2)
+        for c in range(F_PASSES - 1):
+            second_passes(1, 1, c, first_bank=0)
+        weigh(1, 3)
+        quantize_y(0, 1)
+        quantize_loss(1, 3)
+        second_passes(1, 0, 3)
+        second_passes(1, 1, 3)
+        for t in range(PACK):
+            finish(1, 0, t)
+        round_y(1, 0)
+        for t in range(PACK):
+            finish(1, 1, t)
+        round_y(1, 1, split=192)
+        quantize_y(1, 0)
+        quantize_y(1, 1)

@@ -25,6 +25,7 @@ K_PASSES = K // PASS
 F_PASSES = F // PASS
 N_HALVES = N // PASS
 RUN = 4
+PAIR = 2
 
 
 def tile_correlated_insurer_losses_h1_kernel(
@@ -49,29 +50,36 @@ def tile_correlated_insurer_losses_h1_kernel(
         h_words = keep.tile([P, F_PASSES, 2 * N], U8, align_bytes=64)
         h_sc = keep.tile([P, F_PASSES, N], U8, align_bytes=64)
         sev = keep.tile([P, F_PASSES, PACK], BF16, align_bytes=64)
+        sev32 = keep.tile([P, F_PASSES, PACK], F32, align_bytes=64)
         index = keep.tile([P, HALVES, PACK], BF16, align_bytes=64)
         cost = keep.tile([P, N], BF16, align_bytes=64)
         loss_codes = keep.tile([P, HALVES, F_PASSES, PASS], U32, align_bytes=64)
         loss_sc = keep.tile([P, HALVES, F_PASSES, PASS], U8, align_bytes=64)
         y_codes = keep.tile([P, HALVES, N], U32, align_bytes=64)
         y_sc = keep.tile([P, HALVES, N], U8, align_bytes=64)
-        warm = keep.tile([P, 2], F32, align_bytes=64)
 
         live = {}
 
-        def bank(number, shape):
-            return psum.tile(shape, F32, name="bank%d" % number, tag="bank%d" % number)
+        free_banks = list(range(8))
 
-        def load_draws(h, g):
-            rows = draws[h * PASS : (h + 1) * PASS, g * PASS : (g + 1) * PASS]
-            nc.sync.dma_start(out=draws_raw[:, h, g, :, :], in_=rows.rearrange("(m t) k -> m t k", t=PACK))
+        def take_bank(key, shape):
+            number = free_banks.pop(0)
+            live[key] = psum.tile(shape, F32, name="bank%d" % number, tag="bank%d" % number)
+            live["number", key] = number
+            return live[key]
 
-        def load_scale_rows(plane, source):
-            rows = source.bitcast(I32)
+        def give_bank(key):
+            free_banks.append(live["number", key])
+
+        def load_draws(h, g, a):
+            rows = draws[h * PASS : (h + 1) * PASS, g * PASS : (g + 1) * PASS].rearrange("(m t) k -> m t k", t=PACK)
+            nc.sync.dma_start(out=draws_raw[:, h, g, 2 * a : 2 * a + 2, :], in_=rows[:, 2 * a : 2 * a + 2, :])
+
+        def load_scale_rows(plane, source, first, last):
             for q in range(4):
                 nc.sync.dma_start(
-                    out=plane[32 * q : 32 * q + 4, :, :].bitcast(I32),
-                    in_=rows[:, 4 * q : 4 * q + 4, :].rearrange("g r n -> r g n"),
+                    out=plane[32 * q : 32 * q + 4, :, first:last].bitcast(I32),
+                    in_=source[:, 4 * q : 4 * q + 4, first:last].bitcast(I32).rearrange("g r n -> r g n"),
                 )
 
         def load_l(c):
@@ -94,19 +102,20 @@ def tile_correlated_insurer_losses_h1_kernel(
                 in_=l_raw[:, c, :, :].rearrange("p g (m t b) -> p g t m b", t=PACK, b=2),
             )
 
-        def turn_draws(h, g):
-            grouped = work.tile([P, PASS, PACK], BF16, name="grouped", align_bytes=64)
-            live["grouped", h, g] = grouped
-            for a in range(2):
-                turned = bank(4 + 2 * g + a, [P, 2, 2, P])
-                for i in range(2):
-                    words = draws_raw[:, h, g, 2 * a + i, :].bitcast(F32)
-                    for u in range(2):
-                        nc.tensor.transpose(turned[:, i, u, :], words[:, u : 2 * P : 2], ident[:])
-                nc.scalar.copy(
-                    out=grouped[:, 2 * a * P : 2 * (a + 1) * P, :].bitcast(F32).rearrange("p (i r) u -> p i r u", i=2),
-                    in_=turned[:].rearrange("p i u r -> p i r u"),
-                )
+        def turn_draws(h, g, a):
+            if a == 0:
+                live["grouped", h, g] = work.tile([P, PASS, PACK], BF16, name="grouped", align_bytes=64)
+            grouped = live["grouped", h, g]
+            turned = take_bank(("turned", h, g, a), [P, 2, 2, P])
+            for i in range(2):
+                words = draws_raw[:, h, g, 2 * a + i, :].bitcast(F32)
+                for u in range(2):
+                    nc.tensor.transpose(turned[:, i, u, :], words[:, u : 2 * P : 2], ident[:])
+            nc.scalar.copy(
+                out=grouped[:, 2 * a * P : 2 * (a + 1) * P, :].bitcast(F32).rearrange("p (i r) u -> p i r u", i=2),
+                in_=turned[:].rearrange("p i u r -> p i r u"),
+            )
+            give_bank(("turned", h, g, a))
 
         def quantize_draws(h, g):
             nc.vector.quantize_mx(
@@ -116,15 +125,16 @@ def tile_correlated_insurer_losses_h1_kernel(
             )
 
         def first_product(h, c, pass_major=False):
-            prob = work.tile([P, PACK, PASS], F32, name="prob", bufs=4, align_bytes=64)
+            prob = work.tile([P, PACK, PASS], F32, name="prob", bufs=5, align_bytes=64)
             live["prob", h, c] = prob
-            banks = [bank(t, [P, PASS]) for t in range(PACK)]
             order = [(t, g) for t in range(PACK) for g in range(K_PASSES)]
             if pass_major:
                 order = [(t, g) for g in range(K_PASSES) for t in range(PACK)]
             for t, g in order:
+                if g == 0:
+                    take_bank(("x", h, c, t), [P, PASS])
                 nc.tensor.matmul_mx(
-                    out=banks[t][:],
+                    out=live["x", h, c, t][:],
                     lhsT=l_words[:, c, g, 2 * P * t : 2 * P * (t + 1)].bitcast(FP4X4),
                     lhsT_scale=l_sc[:, g, c * PASS + P * t : c * PASS + P * (t + 1)],
                     rhs=draws_codes[:, h, g, :].bitcast(FP8X4),
@@ -133,16 +143,33 @@ def tile_correlated_insurer_losses_h1_kernel(
                     stop=(g == K_PASSES - 1),
                 )
                 if g == K_PASSES - 1:
-                    nc.scalar.activation(out=prob[:, t, :], in_=banks[t][:], func=ACT.Sigmoid, scale=SLOPE)
+                    nc.scalar.activation(out=prob[:, t, :], in_=live["x", h, c, t][:], func=ACT.Sigmoid, scale=SLOPE)
+                    give_bank(("x", h, c, t))
 
         def weigh(h, c):
-            loss = work.tile([P, PASS, PACK], BF16, name="loss", align_bytes=64)
+            loss = work.tile([P, PASS, PACK], BF16, name="loss", bufs=3, align_bytes=64)
             live["loss", h, c] = loss
             nc.vector.tensor_tensor(
-                out=loss[:].rearrange("p (s i) t -> p s t i", i=RUN),
-                in0=live["prob", h, c][:].rearrange("p t (s i) -> p s t i", i=RUN),
-                in1=sev[:, c, :].unsqueeze(1).unsqueeze(3).to_broadcast([P, PASS // RUN, PACK, RUN]),
+                out=loss[:].rearrange("p (s i) t -> p s t i", i=PAIR),
+                in0=live["prob", h, c][:].rearrange("p t (s i) -> p s t i", i=PAIR),
+                in1=sev[:, c, :].unsqueeze(1).unsqueeze(3).to_broadcast([P, PASS // PAIR, PACK, PAIR]),
                 op=ALU.mult,
+            )
+
+        def weigh_rows(h, c):
+            rows = work.tile([P, PACK, PASS], BF16, name="rows", align_bytes=64)
+            live["rows", h, c] = rows
+            for t in range(PACK):
+                nc.scalar.activation(
+                    out=rows[:, t, :], in_=live["prob", h, c][:, t, :], func=ACT.Copy, scale=sev32[:, c, t : t + 1]
+                )
+
+        def group_rows(h, c):
+            loss = work.tile([P, PASS, PACK], BF16, name="loss", bufs=3, align_bytes=64)
+            live["loss", h, c] = loss
+            nc.vector.tensor_copy(
+                out=loss[:].rearrange("p (s i) t -> p s t i", i=RUN),
+                in_=live["rows", h, c][:].rearrange("p t (s i) -> p s t i", i=RUN),
             )
 
         def quantize_loss(h, c):
@@ -152,9 +179,9 @@ def tile_correlated_insurer_losses_h1_kernel(
                 in_=live["loss", h, c][:].rearrange("p s t -> p (s t)"),
             )
 
-        def second_pass(h, j, t, c, first_bank=4):
+        def second_pass(h, j, t, c):
             if c == 0:
-                live["net", h, j, t] = bank(first_bank + t, [P, PASS])
+                take_bank(("net", h, j, t), [P, PASS])
             nc.tensor.matmul_mx(
                 out=live["net", h, j, t][:],
                 lhsT=loss_codes[:, h, c, P * t : P * (t + 1)].bitcast(FP8X4),
@@ -165,140 +192,187 @@ def tile_correlated_insurer_losses_h1_kernel(
                 stop=(c == F_PASSES - 1),
             )
 
-        def second_passes(h, j, c, first_bank=4):
+        def second_passes(h, j, c):
             for t in range(PACK):
-                second_pass(h, j, t, c, first_bank)
+                second_pass(h, j, t, c)
 
-        def finish(h, j, t):
+        def second_bank(h, j, t):
+            for c in range(F_PASSES):
+                second_pass(h, j, t, c)
+
+        def finish(h, j, t, first=0, last=PASS, key=None):
             if t == 0:
-                live["y", h, j] = work.tile([P, PACK, PASS], F32, name="y", bufs=3, align_bytes=64)
+                live["y", h, j] = work.tile([P, PACK, PASS], F32, name="y", bufs=4, align_bytes=64)
+                live["rounded", h, j] = None
+            key = key or ("net", h, j, t)
             y = live["y", h, j]
-            cols = slice(j * PASS, (j + 1) * PASS)
+            cols = slice(j * PASS + first, j * PASS + last)
             nc.vector.scalar_tensor_tensor(
-                out=y[:, t, :], in0=live["net", h, j, t][:], scalar=index[:, h, t : t + 1], in1=cost[:, cols],
+                out=y[:, t, first:last], in0=live[key][:], scalar=index[:, h, t : t + 1], in1=cost[:, cols],
                 op0=ALU.mult, op1=ALU.add,
             )
-            rows = out_0[h * PASS : (h + 1) * PASS, cols].rearrange("(p t) n -> p t n", t=PACK)
-            nc.sync.dma_start(out=rows[:, t, :], in_=y[:, t, :])
+            give_bank(key)
 
-        def round_y(h, j, split=PASS):
-            y = live["y", h, j]
-            rounded = work.tile([P, PASS, PACK], BF16, name="rounded", align_bytes=64)
-            live["rounded", h, j] = rounded
-            nc.scalar.copy(
-                out=rounded[:, :split, :].rearrange("p (n i) t -> p n t i", i=RUN),
-                in_=y[:, :, :split].rearrange("p t (n i) -> p n t i", i=RUN),
-            )
-            if split < PASS:
-                nc.vector.tensor_copy(
-                    out=rounded[:, split:, :].rearrange("p (n i) t -> p n t i", i=RUN),
-                    in_=y[:, :, split:].rearrange("p t (n i) -> p n t i", i=RUN),
+        def store_y(h, j, t):
+            rows = out_0[h * PASS : (h + 1) * PASS, j * PASS : (j + 1) * PASS].rearrange("(p t) n -> p t n", t=PACK)
+            nc.sync.dma_start(out=rows[:, t, :], in_=live["y", h, j][:, t, :])
+
+        def finish_store(h, j, t):
+            finish(h, j, t)
+            store_y(h, j, t)
+
+        def narrow_bank(h, j, t, i):
+            net = take_bank(("narrow", i), [P, P])
+            first = PASS * j + P * i
+            for c in range(F_PASSES):
+                nc.tensor.matmul_mx(
+                    out=net[:],
+                    lhsT=loss_codes[:, h, c, P * t : P * (t + 1)].bitcast(FP8X4),
+                    lhsT_scale=loss_sc[:, h, c, P * t : P * (t + 1)],
+                    rhs=h_words[:, c, 2 * first : 2 * (first + P)].bitcast(FP4X4),
+                    rhs_scale=h_sc[:, c, first : first + P],
+                    start=(c == 0),
+                    stop=(c == F_PASSES - 1),
                 )
 
-        def quantize_y(h, j):
-            cols = slice(j * PASS, (j + 1) * PASS)
+        def round_y(h, j, copy, first=0, last=PASS):
+            if live["rounded", h, j] is None:
+                live["rounded", h, j] = work.tile([P, PASS, PACK], BF16, name="rounded", align_bytes=64)
+            copy(
+                out=live["rounded", h, j][:, first:last, :].rearrange("p (n i) t -> p n t i", i=RUN),
+                in_=live["y", h, j][:, :, first:last].rearrange("p t (n i) -> p n t i", i=RUN),
+            )
+
+        def quantize_y(h, j, first=0, last=PASS):
+            cols = slice(j * PASS + first, j * PASS + last)
             nc.vector.quantize_mx(
                 out=y_codes[:, h, cols].bitcast(FP8X4),
                 scales=y_sc[:, h, cols],
-                in_=live["rounded", h, j][:].rearrange("p n t -> p (n t)"),
+                in_=live["rounded", h, j][:, first:last, :].rearrange("p n t -> p (n t)"),
             )
+
+        def store_words(h, first, last):
             words = out_1[h].rearrange("p n t -> p (n t)").bitcast(I32)
-            nc.sync.dma_start(out=words[:, cols], in_=y_codes[:, h, cols].bitcast(I32))
-            if j == N_HALVES - 1:
-                rows = out_2[h].bitcast(I32)
-                for q in range(4):
-                    nc.sync.dma_start(out=rows[4 * q : 4 * q + 4, :], in_=y_sc[32 * q : 32 * q + 4, h, :].bitcast(I32))
+            nc.sync.dma_start(out=words[:, first:last], in_=y_codes[:, h, first:last].bitcast(I32))
+
+        def store_scales(h, queue):
+            rows = out_2[h].bitcast(I32)
+            for q in range(4):
+                queue.dma_start(out=rows[4 * q : 4 * q + 4, :], in_=y_sc[32 * q : 32 * q + 4, h, :].bitcast(I32))
 
         nc.vector.memset(l_sc_raw[:].bitcast(I32), 0)
         nc.vector.memset(h_sc[:].bitcast(I32), 0)
         make_identity(nc, ident[:])
-        nc.scalar.activation(out=warm[:], in_=ident[:, 0:2], func=ACT.Sigmoid, scale=SLOPE)
 
-        load_draws(0, 0)
+        load_draws(0, 0, 0)
+        load_draws(0, 0, 1)
         load_l(0)
-        load_scale_rows(l_sc_raw, factor_scales)
-        load_draws(0, 1)
+        load_scale_rows(l_sc_raw, factor_scales, 0, PASS)
+        load_draws(0, 1, 0)
+        load_draws(0, 1, 1)
         load_l(1)
-        load_draws(1, 0)
+        load_scale_rows(l_sc_raw, factor_scales, PASS, F)
         nc.sync.dma_start(out=sev[:], in_=severity.rearrange("(c p t) -> p c t", p=P, t=PACK))
+        load_draws(1, 0, 0)
+        load_draws(1, 0, 1)
         load_l(2)
-        load_draws(1, 1)
+        load_draws(1, 1, 0)
+        load_draws(1, 1, 1)
         load_l(3)
-        load_scale_rows(h_sc, shares_scales)
+        load_scale_rows(h_sc, shares_scales, 0, N)
         for c in range(F_PASSES):
             load_h(c)
         nc.sync.dma_start(out=index[:], in_=claims_index.rearrange("(h p t) -> p h t", p=P, t=PACK))
         nc.sync.dma_start(out=cost[:], in_=expense.partition_broadcast(P))
 
-        turn_draws(0, 0)
-        turn_draws(0, 1)
+        for g in range(K_PASSES):
+            for a in range(2):
+                turn_draws(0, g, a)
         permute_l(0)
         permute_sc(0)
         quantize_draws(0, 0)
-        permute_sc(1)
         permute_l(1)
         quantize_draws(0, 1)
+        permute_sc(1)
         permute_sc(2)
         permute_l(2)
         permute_sc(3)
         permute_l(3)
+        nc.scalar.copy(out=sev32[:], in_=sev[:])
         first_product(0, 0, pass_major=True)
-        turn_draws(1, 0)
         first_product(0, 1)
-        turn_draws(1, 1)
+        turn_draws(1, 0, 0)
+        turn_draws(1, 0, 1)
+        turn_draws(1, 1, 0)
+        turn_draws(1, 1, 1)
+        first_product(0, 2)
         weigh(0, 0)
         quantize_draws(1, 0)
         quantize_loss(0, 0)
-        first_product(0, 2)
-        second_passes(0, 0, 0)
+        first_product(0, 3)
         weigh(0, 1)
         quantize_draws(1, 1)
         quantize_loss(0, 1)
-        first_product(0, 3)
-        second_passes(0, 0, 1)
-        weigh(0, 2)
-        quantize_loss(0, 2)
         first_product(1, 0)
-        second_passes(0, 0, 2)
-        weigh(0, 3)
-        quantize_loss(0, 3)
+        weigh(0, 2)
         first_product(1, 1)
-        second_passes(0, 0, 3)
-        weigh(1, 0)
-        finish(0, 0, 0)
-        quantize_loss(1, 0)
-        for t in range(1, PACK):
-            finish(0, 0, t)
+        weigh(0, 3)
+        quantize_loss(0, 2)
         first_product(1, 2)
-        for t in range(PACK):
-            for c in range(F_PASSES):
-                second_pass(0, 1, t, c)
-        round_y(0, 0)
-        weigh(1, 1)
-        finish(0, 1, 0)
-        quantize_loss(1, 1)
-        for t in range(1, PACK):
-            finish(0, 1, t)
+        weigh(1, 0)
+        quantize_loss(0, 3)
         first_product(1, 3)
-        second_passes(1, 0, 0)
-        second_passes(1, 0, 1)
-        round_y(0, 1)
-        weigh(1, 2)
-        quantize_y(0, 0)
+        weigh(1, 1)
+        quantize_loss(1, 0)
+        weigh_rows(1, 2)
+        weigh_rows(1, 3)
+        for t in range(PACK):
+            second_bank(0, 0, t)
+        for t in range(PACK):
+            second_bank(0, 1, t)
+        finish_store(0, 0, 0)
+        quantize_loss(1, 1)
+        finish_store(0, 0, 1)
+        group_rows(1, 2)
+        finish_store(0, 0, 2)
         quantize_loss(1, 2)
-        second_passes(1, 0, 2)
-        for c in range(F_PASSES - 1):
-            second_passes(1, 1, c, first_bank=0)
-        weigh(1, 3)
-        quantize_y(0, 1)
+        group_rows(1, 3)
+        finish_store(0, 0, 3)
         quantize_loss(1, 3)
-        second_passes(1, 0, 3)
-        second_passes(1, 1, 3)
+        round_y(0, 0, nc.scalar.copy)
         for t in range(PACK):
-            finish(1, 0, t)
-        round_y(1, 0)
+            second_bank(1, 0, t)
         for t in range(PACK):
-            finish(1, 1, t)
-        round_y(1, 1, split=192)
+            finish_store(0, 1, t)
+        round_y(0, 1, nc.scalar.copy)
+        for t in range(PACK - 1):
+            second_bank(1, 1, t)
+        quantize_y(0, 0)
+        store_words(0, 0, PASS)
+        for t in range(PACK):
+            finish_store(1, 0, t)
+        round_y(1, 0, nc.scalar.copy)
+        for i in range(PACK):
+            narrow_bank(1, 1, PACK - 1, i)
+        quantize_y(0, 1)
+        store_words(0, PASS, N)
+        store_scales(0, nc.sync)
+        finish_store(1, 1, 0)
+        finish_store(1, 1, 1)
         quantize_y(1, 0)
-        quantize_y(1, 1)
+        store_words(1, 0, PASS)
+        finish_store(1, 1, 2)
+        finish(1, 1, 3, 0, P, ("narrow", 0))
+        round_y(1, 1, nc.scalar.copy, 0, P)
+        finish(1, 1, 3, P, 2 * P, ("narrow", 1))
+        finish(1, 1, 3, 2 * P, 3 * P, ("narrow", 2))
+        round_y(1, 1, nc.scalar.copy, 2 * P, 3 * P)
+        round_y(1, 1, nc.vector.tensor_copy, P, 2 * P)
+        finish(1, 1, 3, 3 * P, 4 * P, ("narrow", 3))
+        store_y(1, 1, 3)
+        quantize_y(1, 1, 0, 2 * P)
+        store_words(1, PASS, PASS + 2 * P)
+        round_y(1, 1, nc.vector.tensor_copy, 3 * P, 4 * P)
+        quantize_y(1, 1, 2 * P, 4 * P)
+        store_words(1, PASS + 2 * P, N)
+        store_scales(1, nc.scalar)

@@ -255,10 +255,10 @@ def tile_correlated_insurer_losses_h1_kernel(
             words = out_1[h].rearrange("p n t -> p (n t)").bitcast(I32)
             nc.sync.dma_start(out=words[:, first:last], in_=y_codes[:, h, first:last].bitcast(I32))
 
-        def store_scales(h, queue):
+        def store_scales(h, queues):
             rows = out_2[h].bitcast(I32)
             for q in range(4):
-                queue.dma_start(out=rows[4 * q : 4 * q + 4, :], in_=y_sc[32 * q : 32 * q + 4, h, :].bitcast(I32))
+                queues[q % 2].dma_start(out=rows[4 * q : 4 * q + 4, :], in_=y_sc[32 * q : 32 * q + 4, h, :].bitcast(I32))
 
         nc.vector.memset(l_sc_raw[:].bitcast(I32), 0)
         nc.vector.memset(h_sc[:].bitcast(I32), 0)
@@ -300,9 +300,9 @@ def tile_correlated_insurer_losses_h1_kernel(
         permute_l(3)
         nc.scalar.copy(out=sev32[:], in_=sev[:])
         first_product(0, 0, pass_major=True)
-        first_product(0, 1)
         turn_draws(1, 0, 0)
         turn_draws(1, 0, 1)
+        first_product(0, 1)
         turn_draws(1, 1, 0)
         turn_draws(1, 1, 1)
         first_product(0, 2)
@@ -333,17 +333,21 @@ def tile_correlated_insurer_losses_h1_kernel(
         finish_store(0, 0, 0)
         quantize_loss(1, 1)
         finish_store(0, 0, 1)
-        group_rows(1, 2)
         finish_store(0, 0, 2)
+        finish_store(0, 0, 3)
+        group_rows(1, 2)
+        finish_store(0, 1, 0)
         quantize_loss(1, 2)
         group_rows(1, 3)
-        finish_store(0, 0, 3)
+        finish_store(0, 1, 1)
         quantize_loss(1, 3)
         round_y(0, 0, nc.scalar.copy)
-        for t in range(PACK):
-            second_bank(1, 0, t)
-        for t in range(PACK):
-            finish_store(0, 1, t)
+        for c in range(F_PASSES):
+            for t in range(3):
+                second_pass(1, 0, t, c)
+        second_bank(1, 0, 3)
+        finish_store(0, 1, 2)
+        finish_store(0, 1, 3)
         round_y(0, 1, nc.scalar.copy)
         for t in range(PACK - 1):
             second_bank(1, 1, t)
@@ -351,16 +355,17 @@ def tile_correlated_insurer_losses_h1_kernel(
         store_words(0, 0, PASS)
         for t in range(PACK):
             finish_store(1, 0, t)
-        round_y(1, 0, nc.scalar.copy)
+        round_y(1, 0, nc.scalar.copy, 0, 320)
         for i in range(PACK):
             narrow_bank(1, 1, PACK - 1, i)
         quantize_y(0, 1)
         store_words(0, PASS, N)
-        store_scales(0, nc.sync)
+        store_scales(0, (nc.sync, nc.sync))
+        round_y(1, 0, nc.vector.tensor_copy, 320, PASS)
         finish_store(1, 1, 0)
-        finish_store(1, 1, 1)
         quantize_y(1, 0)
         store_words(1, 0, PASS)
+        finish_store(1, 1, 1)
         finish_store(1, 1, 2)
         finish(1, 1, 3, 0, P, ("narrow", 0))
         round_y(1, 1, nc.scalar.copy, 0, P)
@@ -375,4 +380,4 @@ def tile_correlated_insurer_losses_h1_kernel(
         round_y(1, 1, nc.vector.tensor_copy, 3 * P, 4 * P)
         quantize_y(1, 1, 2 * P, 4 * P)
         store_words(1, PASS + 2 * P, N)
-        store_scales(1, nc.scalar)
+        store_scales(1, (nc.scalar, nc.sync))

@@ -20,12 +20,19 @@ ACT = mybir.ActivationFunctionType
 P = 128
 PACK = 4
 PASS = P * PACK
-HALVES = S // PASS
-K_PASSES = K // PASS
-F_PASSES = F // PASS
-N_HALVES = N // PASS
-RUN = 4
-PAIR = 2
+SCENARIO_GROUPS = S // PASS
+DRIVER_GROUPS = K // PASS
+RISK_GROUPS = F // PASS
+FP4_BYTES = 2
+QUADRANTS = 4
+SCALE_ROWS = 4
+BANKS = 8
+COPY_RUN = 4
+MULT_RUN = 2
+PROB_BUFS = 6
+LOSS_BUFS = 3
+Y_BUFS = 4
+SCALAR_ROUND_COLUMNS = 320
 
 
 def tile_correlated_insurer_losses_h1_kernel(
@@ -40,82 +47,113 @@ def tile_correlated_insurer_losses_h1_kernel(
         ctx.enter_context(tc.manual_schedule())
 
         ident = keep.tile([P, P], F32, align_bytes=64)
-        draws_raw = keep.tile([P, HALVES, K_PASSES, PACK, PASS], BF16, align_bytes=64)
-        draws_codes = keep.tile([P, HALVES, K_PASSES, PASS], U32, align_bytes=64)
-        draws_sc = keep.tile([P, HALVES, K_PASSES, PASS], U8, align_bytes=64)
-        l_raw = keep.tile([P, F_PASSES, K_PASSES, 2 * PASS], U8, align_bytes=64)
-        l_words = keep.tile([P, F_PASSES, K_PASSES, 2 * PASS], U8, align_bytes=64)
-        l_sc_raw = keep.tile([P, K_PASSES, F], U8, align_bytes=64)
-        l_sc = keep.tile([P, K_PASSES, F], U8, align_bytes=64)
-        h_words = keep.tile([P, F_PASSES, 2 * N], U8, align_bytes=64)
-        h_sc = keep.tile([P, F_PASSES, N], U8, align_bytes=64)
-        sev = keep.tile([P, F_PASSES, PACK], BF16, align_bytes=64)
-        sev32 = keep.tile([P, F_PASSES, PACK], F32, align_bytes=64)
-        index = keep.tile([P, HALVES, PACK], BF16, align_bytes=64)
+        draws_raw = keep.tile([P, SCENARIO_GROUPS, DRIVER_GROUPS, PACK, PASS], BF16, align_bytes=64)
+        draws_codes = keep.tile([P, SCENARIO_GROUPS, DRIVER_GROUPS, PASS], U32, align_bytes=64)
+        draws_sc = keep.tile([P, SCENARIO_GROUPS, DRIVER_GROUPS, PASS], U8, align_bytes=64)
+        l_raw = keep.tile([P, RISK_GROUPS, DRIVER_GROUPS, FP4_BYTES * PASS], U8, align_bytes=64)
+        l_words = keep.tile([P, RISK_GROUPS, DRIVER_GROUPS, FP4_BYTES * PASS], U8, align_bytes=64)
+        first_sc_raw = keep.tile([P, DRIVER_GROUPS, PASS], U8, align_bytes=64)
+        first_sc = keep.tile([P, DRIVER_GROUPS, PASS], U8, align_bytes=64)
+        rest_sc_raw = keep.tile([P, F - PASS], U8, align_bytes=64)
+        rest_sc = keep.tile([P, DRIVER_GROUPS, F - PASS], U8, align_bytes=64)
+        h_words = keep.tile([P, RISK_GROUPS, FP4_BYTES * N], U8, align_bytes=64)
+        h_sc = keep.tile([P, RISK_GROUPS, N], U8, align_bytes=64)
+        sev = keep.tile([P, RISK_GROUPS, PACK], BF16, align_bytes=64)
+        sev32 = keep.tile([P, RISK_GROUPS, PACK], F32, align_bytes=64)
+        index = keep.tile([P, SCENARIO_GROUPS, PACK], BF16, align_bytes=64)
         cost = keep.tile([P, N], BF16, align_bytes=64)
-        loss_codes = keep.tile([P, HALVES, F_PASSES, PASS], U32, align_bytes=64)
-        loss_sc = keep.tile([P, HALVES, F_PASSES, PASS], U8, align_bytes=64)
-        y_codes = keep.tile([P, HALVES, N], U32, align_bytes=64)
-        y_sc = keep.tile([P, HALVES, N], U8, align_bytes=64)
+        loss_codes = keep.tile([P, SCENARIO_GROUPS, RISK_GROUPS, PASS], U32, align_bytes=64)
+        loss_sc = keep.tile([P, SCENARIO_GROUPS, RISK_GROUPS, PASS], U8, align_bytes=64)
+        y_codes = keep.tile([P, SCENARIO_GROUPS, N], U32, align_bytes=64)
+        y_sc = keep.tile([P, SCENARIO_GROUPS, N], U8, align_bytes=64)
 
         live = {}
-
-        free_banks = list(range(8))
+        bank_of = {}
+        free_banks = list(range(BANKS))
 
         def take_bank(key, shape):
-            number = free_banks.pop(0)
-            live[key] = psum.tile(shape, F32, name="bank%d" % number, tag="bank%d" % number)
-            live["number", key] = number
+            bank_of[key] = free_banks.pop(0)
+            name = "bank%d" % bank_of[key]
+            live[key] = psum.tile(shape, F32, name=name, tag=name)
             return live[key]
 
         def give_bank(key):
-            free_banks.append(live["number", key])
+            free_banks.append(bank_of[key])
 
-        def load_draws(h, g, a):
+        def scale_rows(q, offset=0):
+            return slice(32 * q + offset, 32 * q + offset + SCALE_ROWS)
+
+        def source_rows(q):
+            return slice(SCALE_ROWS * q, SCALE_ROWS * (q + 1))
+
+        def load_draws(h, g, pair):
             rows = draws[h * PASS : (h + 1) * PASS, g * PASS : (g + 1) * PASS].rearrange("(m t) k -> m t k", t=PACK)
-            nc.sync.dma_start(out=draws_raw[:, h, g, 2 * a : 2 * a + 2, :], in_=rows[:, 2 * a : 2 * a + 2, :])
+            slots = slice(2 * pair, 2 * pair + 2)
+            nc.sync.dma_start(out=draws_raw[:, h, g, slots, :], in_=rows[:, slots, :])
 
-        def load_scale_rows(plane, source, first, last):
-            for q in range(4):
+        def load_scale_rows(tile, source, columns):
+            for q in range(QUADRANTS):
                 nc.sync.dma_start(
-                    out=plane[32 * q : 32 * q + 4, :, first:last].bitcast(I32),
-                    in_=source[:, 4 * q : 4 * q + 4, first:last].bitcast(I32).rearrange("g r n -> r g n"),
+                    out=tile[scale_rows(q), :, :].bitcast(I32),
+                    in_=source[:, source_rows(q), 0:columns].bitcast(I32).rearrange("g r n -> r g n"),
                 )
 
+        def load_rest_scales():
+            for g in range(DRIVER_GROUPS):
+                for q in range(QUADRANTS):
+                    nc.sync.dma_start(
+                        out=rest_sc_raw[scale_rows(q, SCALE_ROWS * g), :].bitcast(I32),
+                        in_=factor_scales[g, source_rows(q), PASS:F].bitcast(I32),
+                    )
+
         def load_l(c):
-            part = factor_words.bitcast(I32)[:, :, c * 256 : (c + 1) * 256]
+            width = FP4_BYTES * PASS // 4
+            part = factor_words.bitcast(I32)[:, :, c * width : (c + 1) * width]
             nc.sync.dma_start(out=l_raw[:, c, :, :].bitcast(I32), in_=part.rearrange("g p w -> p g w"))
 
-        def load_h(c):
-            nc.sync.dma_start(out=h_words[:, c, :].bitcast(I32), in_=shares_words.bitcast(I32)[c])
-
-        def permute_sc(c):
-            cols = slice(c * PASS, (c + 1) * PASS)
+        def permute_first_scales():
             nc.vector.tensor_copy(
-                out=l_sc[:, :, cols].rearrange("p g (t m) -> p g t m", t=PACK),
-                in_=l_sc_raw[:, :, cols].rearrange("p g (m t) -> p g t m", t=PACK),
+                out=first_sc[:].rearrange("p g (t m) -> p g t m", t=PACK),
+                in_=first_sc_raw[:].rearrange("p g (m t) -> p g t m", t=PACK),
             )
 
-        def permute_l(c):
+        def permute_rest_scales():
             nc.vector.tensor_copy(
-                out=l_words[:, c, :, :].rearrange("p g (t m b) -> p g t m b", t=PACK, b=2),
-                in_=l_raw[:, c, :, :].rearrange("p g (m t b) -> p g t m b", t=PACK, b=2),
+                out=rest_sc[:, 0, :].rearrange("p (c t m) -> p t c m", t=PACK, m=P),
+                in_=rest_sc_raw[:].rearrange("p (c m t) -> p t c m", t=PACK, m=P),
+            )
+            for q in range(QUADRANTS):
+                nc.sync.dma_start(
+                    out=rest_sc[scale_rows(q), 1, :].bitcast(I32),
+                    in_=rest_sc[scale_rows(q, SCALE_ROWS), 0, :].bitcast(I32),
+                )
+
+        def factor_scale(c, g, t):
+            if c == 0:
+                return first_sc[:, g, P * t : P * (t + 1)]
+            return rest_sc[:, g, (c - 1) * PASS + P * t : (c - 1) * PASS + P * (t + 1)]
+
+        def permute_l(c, first=0, last=DRIVER_GROUPS):
+            nc.vector.tensor_copy(
+                out=l_words[:, c, first:last, :].rearrange("p g (t m b) -> p g t m b", t=PACK, b=FP4_BYTES),
+                in_=l_raw[:, c, first:last, :].rearrange("p g (m t b) -> p g t m b", t=PACK, b=FP4_BYTES),
             )
 
-        def turn_draws(h, g, a):
-            if a == 0:
-                live["grouped", h, g] = work.tile([P, PASS, PACK], BF16, name="grouped", align_bytes=64)
-            grouped = live["grouped", h, g]
-            turned = take_bank(("turned", h, g, a), [P, 2, 2, P])
-            for i in range(2):
-                words = draws_raw[:, h, g, 2 * a + i, :].bitcast(F32)
-                for u in range(2):
-                    nc.tensor.transpose(turned[:, i, u, :], words[:, u : 2 * P : 2], ident[:])
-            nc.scalar.copy(
-                out=grouped[:, 2 * a * P : 2 * (a + 1) * P, :].bitcast(F32).rearrange("p (i r) u -> p i r u", i=2),
-                in_=turned[:].rearrange("p i u r -> p i r u"),
-            )
-            give_bank(("turned", h, g, a))
+        def turn_draws(h, g):
+            grouped = work.tile([P, PASS, PACK], BF16, name="grouped", align_bytes=64)
+            live["grouped", h, g] = grouped
+            for pair in range(2):
+                turned = take_bank(("turned", h, g, pair), [P, 2, 2, P])
+                for i in range(2):
+                    words = draws_raw[:, h, g, 2 * pair + i, :].bitcast(F32)
+                    for u in range(2):
+                        nc.tensor.transpose(turned[:, i, u, :], words[:, u : 2 * P : 2], ident[:])
+                columns = slice(2 * pair * P, 2 * (pair + 1) * P)
+                nc.scalar.copy(
+                    out=grouped[:, columns, :].bitcast(F32).rearrange("p (i m) u -> p i m u", i=2),
+                    in_=turned[:].rearrange("p i u m -> p i m u"),
+                )
+                give_bank(("turned", h, g, pair))
 
         def quantize_draws(h, g):
             nc.vector.quantize_mx(
@@ -124,35 +162,44 @@ def tile_correlated_insurer_losses_h1_kernel(
                 in_=live["grouped", h, g][:].rearrange("p s t -> p (s t)"),
             )
 
-        def first_product(h, c, pass_major=False):
-            prob = work.tile([P, PACK, PASS], F32, name="prob", bufs=5, align_bytes=64)
-            live["prob", h, c] = prob
-            order = [(t, g) for t in range(PACK) for g in range(K_PASSES)]
-            if pass_major:
-                order = [(t, g) for g in range(K_PASSES) for t in range(PACK)]
-            for t, g in order:
-                if g == 0:
-                    take_bank(("x", h, c, t), [P, PASS])
-                nc.tensor.matmul_mx(
-                    out=live["x", h, c, t][:],
-                    lhsT=l_words[:, c, g, 2 * P * t : 2 * P * (t + 1)].bitcast(FP4X4),
-                    lhsT_scale=l_sc[:, g, c * PASS + P * t : c * PASS + P * (t + 1)],
-                    rhs=draws_codes[:, h, g, :].bitcast(FP8X4),
-                    rhs_scale=draws_sc[:, h, g, :],
-                    start=(g == 0),
-                    stop=(g == K_PASSES - 1),
+        def first_pass(h, c, t, g):
+            if g == 0:
+                take_bank(("x", h, c, t), [P, PASS])
+            nc.tensor.matmul_mx(
+                out=live["x", h, c, t][:],
+                lhsT=l_words[:, c, g, FP4_BYTES * P * t : FP4_BYTES * P * (t + 1)].bitcast(FP4X4),
+                lhsT_scale=factor_scale(c, g, t),
+                rhs=draws_codes[:, h, g, :].bitcast(FP8X4),
+                rhs_scale=draws_sc[:, h, g, :],
+                start=(g == 0),
+                stop=(g == DRIVER_GROUPS - 1),
+            )
+            if g == DRIVER_GROUPS - 1:
+                if t == 0:
+                    live["prob", h, c] = work.tile([P, PACK, PASS], F32, name="prob", bufs=PROB_BUFS, align_bytes=64)
+                nc.scalar.activation(
+                    out=live["prob", h, c][:, t, :], in_=live["x", h, c, t][:], func=ACT.Sigmoid, scale=SLOPE
                 )
-                if g == K_PASSES - 1:
-                    nc.scalar.activation(out=prob[:, t, :], in_=live["x", h, c, t][:], func=ACT.Sigmoid, scale=SLOPE)
-                    give_bank(("x", h, c, t))
+                give_bank(("x", h, c, t))
+
+        def first_passes(h, c, g):
+            for t in range(PACK):
+                first_pass(h, c, t, g)
+
+        def first_product(h, c):
+            for t in range(PACK):
+                for g in range(DRIVER_GROUPS):
+                    first_pass(h, c, t, g)
+
+        def new_loss(h, c):
+            live["loss", h, c] = work.tile([P, PASS, PACK], BF16, name="loss", bufs=LOSS_BUFS, align_bytes=64)
+            return live["loss", h, c]
 
         def weigh(h, c):
-            loss = work.tile([P, PASS, PACK], BF16, name="loss", bufs=3, align_bytes=64)
-            live["loss", h, c] = loss
             nc.vector.tensor_tensor(
-                out=loss[:].rearrange("p (s i) t -> p s t i", i=PAIR),
-                in0=live["prob", h, c][:].rearrange("p t (s i) -> p s t i", i=PAIR),
-                in1=sev[:, c, :].unsqueeze(1).unsqueeze(3).to_broadcast([P, PASS // PAIR, PACK, PAIR]),
+                out=new_loss(h, c)[:].rearrange("p (s i) t -> p s t i", i=MULT_RUN),
+                in0=live["prob", h, c][:].rearrange("p t (s i) -> p s t i", i=MULT_RUN),
+                in1=sev[:, c, :].unsqueeze(1).unsqueeze(3).to_broadcast([P, PASS // MULT_RUN, PACK, MULT_RUN]),
                 op=ALU.mult,
             )
 
@@ -165,11 +212,9 @@ def tile_correlated_insurer_losses_h1_kernel(
                 )
 
         def group_rows(h, c):
-            loss = work.tile([P, PASS, PACK], BF16, name="loss", bufs=3, align_bytes=64)
-            live["loss", h, c] = loss
             nc.vector.tensor_copy(
-                out=loss[:].rearrange("p (s i) t -> p s t i", i=RUN),
-                in_=live["rows", h, c][:].rearrange("p t (s i) -> p s t i", i=RUN),
+                out=new_loss(h, c)[:].rearrange("p (s i) t -> p s t i", i=COPY_RUN),
+                in_=live["rows", h, c][:].rearrange("p t (s i) -> p s t i", i=COPY_RUN),
             )
 
         def quantize_loss(h, c):
@@ -179,39 +224,36 @@ def tile_correlated_insurer_losses_h1_kernel(
                 in_=live["loss", h, c][:].rearrange("p s t -> p (s t)"),
             )
 
-        def second_pass(h, j, t, c):
+        def second_pass(h, j, t, c, first=0, last=PASS):
             if c == 0:
-                take_bank(("net", h, j, t), [P, PASS])
+                take_bank(("net", h, j, t, first), [P, last - first])
+            low, high = PASS * j + first, PASS * j + last
             nc.tensor.matmul_mx(
-                out=live["net", h, j, t][:],
+                out=live["net", h, j, t, first][:],
                 lhsT=loss_codes[:, h, c, P * t : P * (t + 1)].bitcast(FP8X4),
                 lhsT_scale=loss_sc[:, h, c, P * t : P * (t + 1)],
-                rhs=h_words[:, c, 2 * PASS * j : 2 * PASS * (j + 1)].bitcast(FP4X4),
-                rhs_scale=h_sc[:, c, PASS * j : PASS * (j + 1)],
+                rhs=h_words[:, c, FP4_BYTES * low : FP4_BYTES * high].bitcast(FP4X4),
+                rhs_scale=h_sc[:, c, low:high],
                 start=(c == 0),
-                stop=(c == F_PASSES - 1),
+                stop=(c == RISK_GROUPS - 1),
             )
 
-        def second_passes(h, j, c):
-            for t in range(PACK):
-                second_pass(h, j, t, c)
+        def second_bank(h, j, t, first=0, last=PASS):
+            for c in range(RISK_GROUPS):
+                second_pass(h, j, t, c, first, last)
 
-        def second_bank(h, j, t):
-            for c in range(F_PASSES):
-                second_pass(h, j, t, c)
-
-        def finish(h, j, t, first=0, last=PASS, key=None):
+        def finish(h, j, t, first=0, last=PASS):
             if t == 0:
-                live["y", h, j] = work.tile([P, PACK, PASS], F32, name="y", bufs=4, align_bytes=64)
-                live["rounded", h, j] = None
-            key = key or ("net", h, j, t)
-            y = live["y", h, j]
-            cols = slice(j * PASS + first, j * PASS + last)
+                live["y", h, j] = work.tile([P, PACK, PASS], F32, name="y", bufs=Y_BUFS, align_bytes=64)
             nc.vector.scalar_tensor_tensor(
-                out=y[:, t, first:last], in0=live[key][:], scalar=index[:, h, t : t + 1], in1=cost[:, cols],
-                op0=ALU.mult, op1=ALU.add,
+                out=live["y", h, j][:, t, first:last],
+                in0=live["net", h, j, t, first][:],
+                scalar=index[:, h, t : t + 1],
+                in1=cost[:, PASS * j + first : PASS * j + last],
+                op0=ALU.mult,
+                op1=ALU.add,
             )
-            give_bank(key)
+            give_bank(("net", h, j, t, first))
 
         def store_y(h, j, t):
             rows = out_0[h * PASS : (h + 1) * PASS, j * PASS : (j + 1) * PASS].rearrange("(p t) n -> p t n", t=PACK)
@@ -221,163 +263,139 @@ def tile_correlated_insurer_losses_h1_kernel(
             finish(h, j, t)
             store_y(h, j, t)
 
-        def narrow_bank(h, j, t, i):
-            net = take_bank(("narrow", i), [P, P])
-            first = PASS * j + P * i
-            for c in range(F_PASSES):
-                nc.tensor.matmul_mx(
-                    out=net[:],
-                    lhsT=loss_codes[:, h, c, P * t : P * (t + 1)].bitcast(FP8X4),
-                    lhsT_scale=loss_sc[:, h, c, P * t : P * (t + 1)],
-                    rhs=h_words[:, c, 2 * first : 2 * (first + P)].bitcast(FP4X4),
-                    rhs_scale=h_sc[:, c, first : first + P],
-                    start=(c == 0),
-                    stop=(c == F_PASSES - 1),
-                )
-
         def round_y(h, j, copy, first=0, last=PASS):
-            if live["rounded", h, j] is None:
+            if first == 0:
                 live["rounded", h, j] = work.tile([P, PASS, PACK], BF16, name="rounded", align_bytes=64)
             copy(
-                out=live["rounded", h, j][:, first:last, :].rearrange("p (n i) t -> p n t i", i=RUN),
-                in_=live["y", h, j][:, :, first:last].rearrange("p t (n i) -> p n t i", i=RUN),
+                out=live["rounded", h, j][:, first:last, :].rearrange("p (n i) t -> p n t i", i=COPY_RUN),
+                in_=live["y", h, j][:, :, first:last].rearrange("p t (n i) -> p n t i", i=COPY_RUN),
             )
 
-        def quantize_y(h, j, first=0, last=PASS):
-            cols = slice(j * PASS + first, j * PASS + last)
+        def quantize_store_y(h, j, first=0, last=PASS):
+            columns = slice(j * PASS + first, j * PASS + last)
             nc.vector.quantize_mx(
-                out=y_codes[:, h, cols].bitcast(FP8X4),
-                scales=y_sc[:, h, cols],
+                out=y_codes[:, h, columns].bitcast(FP8X4),
+                scales=y_sc[:, h, columns],
                 in_=live["rounded", h, j][:, first:last, :].rearrange("p n t -> p (n t)"),
             )
-
-        def store_words(h, first, last):
             words = out_1[h].rearrange("p n t -> p (n t)").bitcast(I32)
-            nc.sync.dma_start(out=words[:, first:last], in_=y_codes[:, h, first:last].bitcast(I32))
+            nc.sync.dma_start(out=words[:, columns], in_=y_codes[:, h, columns].bitcast(I32))
 
         def store_scales(h, queues):
             rows = out_2[h].bitcast(I32)
-            for q in range(4):
-                queues[q % 2].dma_start(out=rows[4 * q : 4 * q + 4, :], in_=y_sc[32 * q : 32 * q + 4, h, :].bitcast(I32))
+            for q in range(QUADRANTS):
+                queues[q % 2].dma_start(out=rows[source_rows(q), :], in_=y_sc[scale_rows(q), h, :].bitcast(I32))
 
-        nc.vector.memset(l_sc_raw[:].bitcast(I32), 0)
+        nc.vector.memset(first_sc_raw[:].bitcast(I32), 0)
+        nc.vector.memset(rest_sc_raw[:].bitcast(I32), 0)
+        nc.vector.memset(rest_sc[:, 1, :].bitcast(I32), 0)
         nc.vector.memset(h_sc[:].bitcast(I32), 0)
         make_identity(nc, ident[:])
 
         load_draws(0, 0, 0)
-        load_draws(0, 0, 1)
         load_l(0)
-        load_scale_rows(l_sc_raw, factor_scales, 0, PASS)
+        load_draws(0, 0, 1)
+        load_scale_rows(first_sc_raw, factor_scales, PASS)
         load_draws(0, 1, 0)
         load_draws(0, 1, 1)
         load_l(1)
-        load_scale_rows(l_sc_raw, factor_scales, PASS, F)
-        nc.sync.dma_start(out=sev[:], in_=severity.rearrange("(c p t) -> p c t", p=P, t=PACK))
+        load_rest_scales()
         load_draws(1, 0, 0)
         load_draws(1, 0, 1)
+        nc.sync.dma_start(out=sev[:], in_=severity.rearrange("(c p t) -> p c t", p=P, t=PACK))
         load_l(2)
         load_draws(1, 1, 0)
         load_draws(1, 1, 1)
         load_l(3)
-        load_scale_rows(h_sc, shares_scales, 0, N)
-        for c in range(F_PASSES):
-            load_h(c)
+
+        turn_draws(0, 0)
+        turn_draws(0, 1)
+        permute_l(0)
+        permute_first_scales()
+        quantize_draws(0, 0)
+        permute_l(1, 0, 1)
+        quantize_draws(0, 1)
+        permute_rest_scales()
+
+        load_scale_rows(h_sc, shares_scales, N)
+        for c in range(RISK_GROUPS):
+            nc.sync.dma_start(out=h_words[:, c, :].bitcast(I32), in_=shares_words.bitcast(I32)[c])
         nc.sync.dma_start(out=index[:], in_=claims_index.rearrange("(h p t) -> p h t", p=P, t=PACK))
         nc.sync.dma_start(out=cost[:], in_=expense.partition_broadcast(P))
 
-        for g in range(K_PASSES):
-            for a in range(2):
-                turn_draws(0, g, a)
-        permute_l(0)
-        permute_sc(0)
-        quantize_draws(0, 0)
-        permute_l(1)
-        quantize_draws(0, 1)
-        permute_sc(1)
-        permute_sc(2)
+        permute_l(1, 1, 2)
         permute_l(2)
-        permute_sc(3)
-        permute_l(3)
+        first_passes(0, 0, 0)
+        first_passes(0, 0, 1)
+        turn_draws(1, 0)
+        first_passes(0, 1, 0)
+        turn_draws(1, 1)
+        first_passes(0, 1, 1)
         nc.scalar.copy(out=sev32[:], in_=sev[:])
-        first_product(0, 0, pass_major=True)
-        turn_draws(1, 0, 0)
-        turn_draws(1, 0, 1)
-        first_product(0, 1)
-        turn_draws(1, 1, 0)
-        turn_draws(1, 1, 1)
+        permute_l(3)
         first_product(0, 2)
         weigh(0, 0)
         quantize_draws(1, 0)
         quantize_loss(0, 0)
+        quantize_draws(1, 1)
         first_product(0, 3)
         weigh(0, 1)
-        quantize_draws(1, 1)
-        quantize_loss(0, 1)
-        first_product(1, 0)
-        weigh(0, 2)
-        first_product(1, 1)
-        weigh(0, 3)
-        quantize_loss(0, 2)
-        first_product(1, 2)
-        weigh(1, 0)
-        quantize_loss(0, 3)
-        first_product(1, 3)
-        weigh(1, 1)
-        quantize_loss(1, 0)
+        on_vector = [(0, 1), (0, 2), (0, 3), (1, 0), (1, 1)]
+        for c in range(RISK_GROUPS):
+            first_product(1, c)
+            weigh(*on_vector[c + 1])
+            quantize_loss(*on_vector[c])
         weigh_rows(1, 2)
         weigh_rows(1, 3)
-        for t in range(PACK):
-            second_bank(0, 0, t)
-        for t in range(PACK):
-            second_bank(0, 1, t)
+
+        for j in range(N // PASS):
+            for t in range(PACK):
+                second_bank(0, j, t)
         finish_store(0, 0, 0)
         quantize_loss(1, 1)
         finish_store(0, 0, 1)
         finish_store(0, 0, 2)
-        finish_store(0, 0, 3)
         group_rows(1, 2)
-        finish_store(0, 1, 0)
+        finish_store(0, 0, 3)
         quantize_loss(1, 2)
         group_rows(1, 3)
-        finish_store(0, 1, 1)
+        finish_store(0, 1, 0)
         quantize_loss(1, 3)
+        finish_store(0, 1, 1)
         round_y(0, 0, nc.scalar.copy)
-        for c in range(F_PASSES):
-            for t in range(3):
+
+        last_t = PACK - 1
+        for c in range(RISK_GROUPS):
+            for t in range(last_t):
                 second_pass(1, 0, t, c)
-        second_bank(1, 0, 3)
+        second_bank(1, 0, last_t)
         finish_store(0, 1, 2)
         finish_store(0, 1, 3)
         round_y(0, 1, nc.scalar.copy)
-        for t in range(PACK - 1):
+        for t in range(last_t):
             second_bank(1, 1, t)
-        quantize_y(0, 0)
-        store_words(0, 0, PASS)
+        quantize_store_y(0, 0)
         for t in range(PACK):
             finish_store(1, 0, t)
-        round_y(1, 0, nc.scalar.copy, 0, 320)
-        for i in range(PACK):
-            narrow_bank(1, 1, PACK - 1, i)
-        quantize_y(0, 1)
-        store_words(0, PASS, N)
+        round_y(1, 0, nc.scalar.copy, 0, SCALAR_ROUND_COLUMNS)
+        for part in range(PASS // P):
+            second_bank(1, 1, last_t, part * P, (part + 1) * P)
+        quantize_store_y(0, 1)
         store_scales(0, (nc.sync, nc.sync))
-        round_y(1, 0, nc.vector.tensor_copy, 320, PASS)
+        round_y(1, 0, nc.vector.tensor_copy, SCALAR_ROUND_COLUMNS, PASS)
         finish_store(1, 1, 0)
-        quantize_y(1, 0)
-        store_words(1, 0, PASS)
+        quantize_store_y(1, 0)
         finish_store(1, 1, 1)
         finish_store(1, 1, 2)
-        finish(1, 1, 3, 0, P, ("narrow", 0))
+        finish(1, 1, last_t, 0, P)
         round_y(1, 1, nc.scalar.copy, 0, P)
-        finish(1, 1, 3, P, 2 * P, ("narrow", 1))
-        finish(1, 1, 3, 2 * P, 3 * P, ("narrow", 2))
+        finish(1, 1, last_t, P, 2 * P)
+        finish(1, 1, last_t, 2 * P, 3 * P)
         round_y(1, 1, nc.scalar.copy, 2 * P, 3 * P)
         round_y(1, 1, nc.vector.tensor_copy, P, 2 * P)
-        finish(1, 1, 3, 3 * P, 4 * P, ("narrow", 3))
-        store_y(1, 1, 3)
-        quantize_y(1, 1, 0, 2 * P)
-        store_words(1, PASS, PASS + 2 * P)
-        round_y(1, 1, nc.vector.tensor_copy, 3 * P, 4 * P)
-        quantize_y(1, 1, 2 * P, 4 * P)
-        store_words(1, PASS + 2 * P, N)
+        finish(1, 1, last_t, 3 * P, PASS)
+        store_y(1, 1, last_t)
+        quantize_store_y(1, 1, 0, 2 * P)
+        round_y(1, 1, nc.vector.tensor_copy, 3 * P, PASS)
+        quantize_store_y(1, 1, 2 * P, PASS)
         store_scales(1, (nc.scalar, nc.sync))

from contextlib import ExitStack

import concourse.mybir as mybir
from concourse.masks import make_identity

S, K, F, N = 1024, 1024, 2048, 1024
SLOPE = 1.702
FLOPS = 2 * S * K * F + 2 * S * F * N

F32 = mybir.dt.float32
BF16 = mybir.dt.bfloat16
I32 = mybir.dt.int32
U32 = mybir.dt.uint32
U8 = mybir.dt.uint8
FP8X4 = mybir.dt.float8_e4m3fn_x4
FP4X4 = mybir.dt.float4_e2m1fn_x4
ALU = mybir.AluOpType
ACT = mybir.ActivationFunctionType

P = 128
PACK = 4
PASS = P * PACK
SCENARIO_GROUPS = S // PASS
DRIVER_GROUPS = K // PASS
RISK_GROUPS = F // PASS
FP4_BYTES = 2
QUADRANTS = 4
SCALE_ROWS = 4
BANKS = 8
COPY_RUN = 4
MULT_RUN = 2
PROB_BUFS = 6
LOSS_BUFS = 3
Y_BUFS = 4
SCALAR_ROUND_COLUMNS = 320


def tile_correlated_insurer_losses_h1_kernel(
    tc, draws, factor_words, factor_scales, severity, shares_words, shares_scales, claims_index, expense,
    out_0, out_1, out_2,
):
    nc = tc.nc
    with ExitStack() as ctx:
        keep = ctx.enter_context(tc.tile_pool(name="keep", bufs=1))
        work = ctx.enter_context(tc.tile_pool(name="work", bufs=2))
        psum = ctx.enter_context(tc.psum_pool(name="psum", bufs=1))
        ctx.enter_context(tc.manual_schedule())

        ident = keep.tile([P, P], F32, align_bytes=64)
        draws_raw = keep.tile([P, SCENARIO_GROUPS, DRIVER_GROUPS, PACK, PASS], BF16, align_bytes=64)
        draws_codes = keep.tile([P, SCENARIO_GROUPS, DRIVER_GROUPS, PASS], U32, align_bytes=64)
        draws_sc = keep.tile([P, SCENARIO_GROUPS, DRIVER_GROUPS, PASS], U8, align_bytes=64)
        l_raw = keep.tile([P, RISK_GROUPS, DRIVER_GROUPS, FP4_BYTES * PASS], U8, align_bytes=64)
        l_words = keep.tile([P, RISK_GROUPS, DRIVER_GROUPS, FP4_BYTES * PASS], U8, align_bytes=64)
        first_sc_raw = keep.tile([P, DRIVER_GROUPS, PASS], U8, align_bytes=64)
        first_sc = keep.tile([P, DRIVER_GROUPS, PASS], U8, align_bytes=64)
        rest_sc_raw = keep.tile([P, F - PASS], U8, align_bytes=64)
        rest_sc = keep.tile([P, DRIVER_GROUPS, F - PASS], U8, align_bytes=64)
        h_words = keep.tile([P, RISK_GROUPS, FP4_BYTES * N], U8, align_bytes=64)
        h_sc = keep.tile([P, RISK_GROUPS, N], U8, align_bytes=64)
        sev = keep.tile([P, RISK_GROUPS, PACK], BF16, align_bytes=64)
        sev32 = keep.tile([P, RISK_GROUPS, PACK], F32, align_bytes=64)
        index = keep.tile([P, SCENARIO_GROUPS, PACK], BF16, align_bytes=64)
        cost = keep.tile([P, N], BF16, align_bytes=64)
        loss_codes = keep.tile([P, SCENARIO_GROUPS, RISK_GROUPS, PASS], U32, align_bytes=64)
        loss_sc = keep.tile([P, SCENARIO_GROUPS, RISK_GROUPS, PASS], U8, align_bytes=64)
        y_codes = keep.tile([P, SCENARIO_GROUPS, N], U32, align_bytes=64)
        y_sc = keep.tile([P, SCENARIO_GROUPS, N], U8, align_bytes=64)

        live = {}
        bank_of = {}
        free_banks = list(range(BANKS))

        def take_bank(key, shape):
            bank_of[key] = free_banks.pop(0)
            name = "bank%d" % bank_of[key]
            live[key] = psum.tile(shape, F32, name=name, tag=name)
            return live[key]

        def give_bank(key):
            free_banks.append(bank_of[key])

        def scale_rows(q, offset=0):
            return slice(32 * q + offset, 32 * q + offset + SCALE_ROWS)

        def source_rows(q):
            return slice(SCALE_ROWS * q, SCALE_ROWS * (q + 1))

        def load_draws(h, g, pair):
            rows = draws[h * PASS : (h + 1) * PASS, g * PASS : (g + 1) * PASS].rearrange("(m t) k -> m t k", t=PACK)
            slots = slice(2 * pair, 2 * pair + 2)
            nc.sync.dma_start(out=draws_raw[:, h, g, slots, :], in_=rows[:, slots, :])

        def load_scale_rows(tile, source, columns):
            for q in range(QUADRANTS):
                nc.sync.dma_start(
                    out=tile[scale_rows(q), :, :].bitcast(I32),
                    in_=source[:, source_rows(q), 0:columns].bitcast(I32).rearrange("g r n -> r g n"),
                )

        def load_rest_scales():
            for g in range(DRIVER_GROUPS):
                for q in range(QUADRANTS):
                    nc.sync.dma_start(
                        out=rest_sc_raw[scale_rows(q, SCALE_ROWS * g), :].bitcast(I32),
                        in_=factor_scales[g, source_rows(q), PASS:F].bitcast(I32),
                    )

        def load_l(c):
            width = FP4_BYTES * PASS // 4
            part = factor_words.bitcast(I32)[:, :, c * width : (c + 1) * width]
            nc.sync.dma_start(out=l_raw[:, c, :, :].bitcast(I32), in_=part.rearrange("g p w -> p g w"))

        def permute_first_scales():
            nc.vector.tensor_copy(
                out=first_sc[:].rearrange("p g (t m) -> p g t m", t=PACK),
                in_=first_sc_raw[:].rearrange("p g (m t) -> p g t m", t=PACK),
            )

        def permute_rest_scales():
            nc.vector.tensor_copy(
                out=rest_sc[:, 0, :].rearrange("p (c t m) -> p t c m", t=PACK, m=P),
                in_=rest_sc_raw[:].rearrange("p (c m t) -> p t c m", t=PACK, m=P),
            )
            for q in range(QUADRANTS):
                nc.sync.dma_start(
                    out=rest_sc[scale_rows(q), 1, :].bitcast(I32),
                    in_=rest_sc[scale_rows(q, SCALE_ROWS), 0, :].bitcast(I32),
                )

        def factor_scale(c, g, t):
            if c == 0:
                return first_sc[:, g, P * t : P * (t + 1)]
            return rest_sc[:, g, (c - 1) * PASS + P * t : (c - 1) * PASS + P * (t + 1)]

        def permute_l(c, first=0, last=DRIVER_GROUPS):
            nc.vector.tensor_copy(
                out=l_words[:, c, first:last, :].rearrange("p g (t m b) -> p g t m b", t=PACK, b=FP4_BYTES),
                in_=l_raw[:, c, first:last, :].rearrange("p g (m t b) -> p g t m b", t=PACK, b=FP4_BYTES),
            )

        def turn_draws(h, g):
            grouped = work.tile([P, PASS, PACK], BF16, name="grouped", align_bytes=64)
            live["grouped", h, g] = grouped
            for pair in range(2):
                turned = take_bank(("turned", h, g, pair), [P, 2, 2, P])
                for i in range(2):
                    words = draws_raw[:, h, g, 2 * pair + i, :].bitcast(F32)
                    for u in range(2):
                        nc.tensor.transpose(turned[:, i, u, :], words[:, u : 2 * P : 2], ident[:])
                columns = slice(2 * pair * P, 2 * (pair + 1) * P)
                nc.scalar.copy(
                    out=grouped[:, columns, :].bitcast(F32).rearrange("p (i m) u -> p i m u", i=2),
                    in_=turned[:].rearrange("p i u m -> p i m u"),
                )
                give_bank(("turned", h, g, pair))

        def quantize_draws(h, g):
            nc.vector.quantize_mx(
                out=draws_codes[:, h, g, :].bitcast(FP8X4),
                scales=draws_sc[:, h, g, :],
                in_=live["grouped", h, g][:].rearrange("p s t -> p (s t)"),
            )

        def first_pass(h, c, t, g):
            if g == 0:
                take_bank(("x", h, c, t), [P, PASS])
            nc.tensor.matmul_mx(
                out=live["x", h, c, t][:],
                lhsT=l_words[:, c, g, FP4_BYTES * P * t : FP4_BYTES * P * (t + 1)].bitcast(FP4X4),
                lhsT_scale=factor_scale(c, g, t),
                rhs=draws_codes[:, h, g, :].bitcast(FP8X4),
                rhs_scale=draws_sc[:, h, g, :],
                start=(g == 0),
                stop=(g == DRIVER_GROUPS - 1),
            )
            if g == DRIVER_GROUPS - 1:
                if t == 0:
                    live["prob", h, c] = work.tile([P, PACK, PASS], F32, name="prob", bufs=PROB_BUFS, align_bytes=64)
                nc.scalar.activation(
                    out=live["prob", h, c][:, t, :], in_=live["x", h, c, t][:], func=ACT.Sigmoid, scale=SLOPE
                )
                give_bank(("x", h, c, t))

        def first_passes(h, c, g):
            for t in range(PACK):
                first_pass(h, c, t, g)

        def first_product(h, c):
            for t in range(PACK):
                for g in range(DRIVER_GROUPS):
                    first_pass(h, c, t, g)

        def new_loss(h, c):
            live["loss", h, c] = work.tile([P, PASS, PACK], BF16, name="loss", bufs=LOSS_BUFS, align_bytes=64)
            return live["loss", h, c]

        def weigh(h, c):
            nc.vector.tensor_tensor(
                out=new_loss(h, c)[:].rearrange("p (s i) t -> p s t i", i=MULT_RUN),
                in0=live["prob", h, c][:].rearrange("p t (s i) -> p s t i", i=MULT_RUN),
                in1=sev[:, c, :].unsqueeze(1).unsqueeze(3).to_broadcast([P, PASS // MULT_RUN, PACK, MULT_RUN]),
                op=ALU.mult,
            )

        def weigh_rows(h, c):
            rows = work.tile([P, PACK, PASS], BF16, name="rows", align_bytes=64)
            live["rows", h, c] = rows
            for t in range(PACK):
                nc.scalar.activation(
                    out=rows[:, t, :], in_=live["prob", h, c][:, t, :], func=ACT.Copy, scale=sev32[:, c, t : t + 1]
                )

        def group_rows(h, c):
            nc.vector.tensor_copy(
                out=new_loss(h, c)[:].rearrange("p (s i) t -> p s t i", i=COPY_RUN),
                in_=live["rows", h, c][:].rearrange("p t (s i) -> p s t i", i=COPY_RUN),
            )

        def quantize_loss(h, c):
            nc.vector.quantize_mx(
                out=loss_codes[:, h, c, :].bitcast(FP8X4),
                scales=loss_sc[:, h, c, :],
                in_=live["loss", h, c][:].rearrange("p s t -> p (s t)"),
            )

        def second_pass(h, j, t, c, first=0, last=PASS):
            if c == 0:
                take_bank(("net", h, j, t, first), [P, last - first])
            low, high = PASS * j + first, PASS * j + last
            nc.tensor.matmul_mx(
                out=live["net", h, j, t, first][:],
                lhsT=loss_codes[:, h, c, P * t : P * (t + 1)].bitcast(FP8X4),
                lhsT_scale=loss_sc[:, h, c, P * t : P * (t + 1)],
                rhs=h_words[:, c, FP4_BYTES * low : FP4_BYTES * high].bitcast(FP4X4),
                rhs_scale=h_sc[:, c, low:high],
                start=(c == 0),
                stop=(c == RISK_GROUPS - 1),
            )

        def second_bank(h, j, t, first=0, last=PASS):
            for c in range(RISK_GROUPS):
                second_pass(h, j, t, c, first, last)

        def finish(h, j, t, first=0, last=PASS):
            if t == 0:
                live["y", h, j] = work.tile([P, PACK, PASS], F32, name="y", bufs=Y_BUFS, align_bytes=64)
            nc.vector.scalar_tensor_tensor(
                out=live["y", h, j][:, t, first:last],
                in0=live["net", h, j, t, first][:],
                scalar=index[:, h, t : t + 1],
                in1=cost[:, PASS * j + first : PASS * j + last],
                op0=ALU.mult,
                op1=ALU.add,
            )
            give_bank(("net", h, j, t, first))

        def store_y(h, j, t):
            rows = out_0[h * PASS : (h + 1) * PASS, j * PASS : (j + 1) * PASS].rearrange("(p t) n -> p t n", t=PACK)
            nc.sync.dma_start(out=rows[:, t, :], in_=live["y", h, j][:, t, :])

        def finish_store(h, j, t):
            finish(h, j, t)
            store_y(h, j, t)

        def round_y(h, j, copy, first=0, last=PASS):
            if first == 0:
                live["rounded", h, j] = work.tile([P, PASS, PACK], BF16, name="rounded", align_bytes=64)
            copy(
                out=live["rounded", h, j][:, first:last, :].rearrange("p (n i) t -> p n t i", i=COPY_RUN),
                in_=live["y", h, j][:, :, first:last].rearrange("p t (n i) -> p n t i", i=COPY_RUN),
            )

        def quantize_store_y(h, j, first=0, last=PASS):
            columns = slice(j * PASS + first, j * PASS + last)
            nc.vector.quantize_mx(
                out=y_codes[:, h, columns].bitcast(FP8X4),
                scales=y_sc[:, h, columns],
                in_=live["rounded", h, j][:, first:last, :].rearrange("p n t -> p (n t)"),
            )
            words = out_1[h].rearrange("p n t -> p (n t)").bitcast(I32)
            nc.sync.dma_start(out=words[:, columns], in_=y_codes[:, h, columns].bitcast(I32))

        def store_scales(h, queues):
            rows = out_2[h].bitcast(I32)
            for q in range(QUADRANTS):
                queues[q % 2].dma_start(out=rows[source_rows(q), :], in_=y_sc[scale_rows(q), h, :].bitcast(I32))

        nc.vector.memset(first_sc_raw[:].bitcast(I32), 0)
        nc.vector.memset(rest_sc_raw[:].bitcast(I32), 0)
        nc.vector.memset(rest_sc[:, 1, :].bitcast(I32), 0)
        nc.vector.memset(h_sc[:].bitcast(I32), 0)
        make_identity(nc, ident[:])

        load_draws(0, 0, 0)
        load_l(0)
        load_draws(0, 0, 1)
        load_scale_rows(first_sc_raw, factor_scales, PASS)
        load_draws(0, 1, 0)
        load_draws(0, 1, 1)
        load_l(1)
        load_rest_scales()
        load_draws(1, 0, 0)
        load_draws(1, 0, 1)
        nc.sync.dma_start(out=sev[:], in_=severity.rearrange("(c p t) -> p c t", p=P, t=PACK))
        load_l(2)
        load_draws(1, 1, 0)
        load_draws(1, 1, 1)
        load_l(3)

        turn_draws(0, 0)
        turn_draws(0, 1)
        permute_l(0)
        permute_first_scales()
        quantize_draws(0, 0)
        permute_l(1, 0, 1)
        quantize_draws(0, 1)
        permute_rest_scales()

        load_scale_rows(h_sc, shares_scales, N)
        for c in range(RISK_GROUPS):
            nc.sync.dma_start(out=h_words[:, c, :].bitcast(I32), in_=shares_words.bitcast(I32)[c])
        nc.sync.dma_start(out=index[:], in_=claims_index.rearrange("(h p t) -> p h t", p=P, t=PACK))
        nc.sync.dma_start(out=cost[:], in_=expense.partition_broadcast(P))

        permute_l(1, 1, 2)
        permute_l(2)
        first_passes(0, 0, 0)
        first_passes(0, 0, 1)
        turn_draws(1, 0)
        first_passes(0, 1, 0)
        turn_draws(1, 1)
        first_passes(0, 1, 1)
        nc.scalar.copy(out=sev32[:], in_=sev[:])
        permute_l(3)
        first_product(0, 2)
        weigh(0, 0)
        quantize_draws(1, 0)
        quantize_loss(0, 0)
        quantize_draws(1, 1)
        first_product(0, 3)
        weigh(0, 1)
        on_vector = [(0, 1), (0, 2), (0, 3), (1, 0), (1, 1)]
        for c in range(RISK_GROUPS):
            first_product(1, c)
            weigh(*on_vector[c + 1])
            quantize_loss(*on_vector[c])
        weigh_rows(1, 2)
        weigh_rows(1, 3)

        for j in range(N // PASS):
            for t in range(PACK):
                second_bank(0, j, t)
        finish_store(0, 0, 0)
        quantize_loss(1, 1)
        finish_store(0, 0, 1)
        finish_store(0, 0, 2)
        group_rows(1, 2)
        finish_store(0, 0, 3)
        quantize_loss(1, 2)
        group_rows(1, 3)
        finish_store(0, 1, 0)
        quantize_loss(1, 3)
        finish_store(0, 1, 1)
        round_y(0, 0, nc.scalar.copy)

        last_t = PACK - 1
        for c in range(RISK_GROUPS):
            for t in range(last_t):
                second_pass(1, 0, t, c)
        second_bank(1, 0, last_t)
        finish_store(0, 1, 2)
        finish_store(0, 1, 3)
        round_y(0, 1, nc.scalar.copy)
        for t in range(last_t):
            second_bank(1, 1, t)
        quantize_store_y(0, 0)
        for t in range(PACK):
            finish_store(1, 0, t)
        round_y(1, 0, nc.scalar.copy, 0, SCALAR_ROUND_COLUMNS)
        for part in range(PASS // P):
            second_bank(1, 1, last_t, part * P, (part + 1) * P)
        quantize_store_y(0, 1)
        store_scales(0, (nc.sync, nc.sync))
        round_y(1, 0, nc.vector.tensor_copy, SCALAR_ROUND_COLUMNS, PASS)
        finish_store(1, 1, 0)
        quantize_store_y(1, 0)
        finish_store(1, 1, 1)
        finish_store(1, 1, 2)
        finish(1, 1, last_t, 0, P)
        round_y(1, 1, nc.scalar.copy, 0, P)
        finish(1, 1, last_t, P, 2 * P)
        finish(1, 1, last_t, 2 * P, 3 * P)
        round_y(1, 1, nc.scalar.copy, 2 * P, 3 * P)
        round_y(1, 1, nc.vector.tensor_copy, P, 2 * P)
        finish(1, 1, last_t, 3 * P, PASS)
        store_y(1, 1, last_t)
        quantize_store_y(1, 1, 0, 2 * P)
        round_y(1, 1, nc.vector.tensor_copy, 3 * P, PASS)
        quantize_store_y(1, 1, 2 * P, PASS)
        store_scales(1, (nc.scalar, nc.sync))
